import numpy as np
import ml_dtypes


def mxq(x, axis, fmt="e4m3"):
    dtype, down = {"e4m3": (ml_dtypes.float8_e4m3fn, 7), "e5m2": (ml_dtypes.float8_e5m2, 14)}[fmt]
    v = np.moveaxis(np.asarray(x, np.float32).astype(ml_dtypes.bfloat16).astype(np.float64), axis, -1)
    blocks = v.reshape(v.shape[:-1] + (-1, 32))
    amax = np.abs(blocks).max(-1, keepdims=True)
    byte = np.maximum(np.where(amax > 0, np.frexp(amax)[1] - 1 + 127, 0) - down, 1)
    scale = np.exp2(byte - 127.0)
    codes = (blocks / scale).astype(np.float32).astype(dtype).astype(np.float64)
    return np.moveaxis((codes * scale).reshape(v.shape), -1, axis)


WIDE = False


def mx_kscale(k):
    if not WIDE:
        return np.ones(k)
    levels = np.array([10, -10, 5, -5, 0])
    if k % 512:
        return np.exp2(np.random.permutation(np.resize(levels, k // 32))).repeat(32)
    a = np.empty((k // 512, 16))
    for p in range(k // 512):
        a[p, :8] = np.random.permutation(np.resize(levels, 8))
        for g in range(8):
            far = levels[np.abs(levels - a[p, g]) >= 10]
            a[p, g + 8] = far[np.random.randint(len(far))]
    return np.exp2(a.ravel()).repeat(32)


def f64(x):
    return np.asarray(x).astype(np.float64)


def striped(idx):
    return np.tile(idx.reshape(-1, 16).T, (8, 1)).astype(np.uint16)


def unstriped(offs):
    return offs[:16].T.reshape(-1).astype(np.int64)


def pack_weight(w):
    k, n = w.shape
    w = f64(np.asarray(w, np.float32).astype(ml_dtypes.bfloat16)).reshape(k // 32, 32, n)
    amax = np.abs(w).max(1)
    byte = np.clip(np.where(amax > 0, np.frexp(amax)[1] - 1 + 127 - 7, 1), 1, 254)
    scaled = (w * np.exp2(127.0 - byte)[:, None, :]).reshape(k, n).astype(np.float32)
    words = np.ascontiguousarray(scaled.reshape(k // 512, 128, 4, n).transpose(0, 1, 3, 2)).astype(ml_dtypes.float8_e4m3fn).view(np.uint8)
    return words, np.ascontiguousarray(byte.astype(np.uint8).reshape(k // 512, 16, n))


def unpack_weight(words, scales):
    g, p, n, _ = words.shape
    vals = np.ascontiguousarray(words).view(ml_dtypes.float8_e4m3fn).astype(np.float64) * np.repeat(np.exp2(scales.astype(np.float64) - 127.0), 8, axis=1)[..., None]
    return vals.transpose(0, 1, 3, 2).reshape(g * 512, n)


def relu(v):
    return np.maximum(v, 0.0)

def planes(y):
    n, m = y.shape
    v = y.astype(np.float32).astype(ml_dtypes.bfloat16).astype(np.float64).reshape(n // 32, 32, m)
    top = np.abs(v).max(1)
    byte = np.clip(np.where(top > 0, np.frexp(top)[1] - 1 + 127 - 7, 1), 1, 254)
    codes = (v * np.exp2(127.0 - byte)[:, None, :]).reshape(n, m).astype(np.float32).astype(ml_dtypes.float8_e4m3fn).view(np.uint8)
    words = codes.reshape(n // 512, 128, 4, m).transpose(0, 1, 3, 2)
    return np.ascontiguousarray(words), np.ascontiguousarray(byte.astype(np.uint8).reshape(n // 512, 16, m))


K, T, D, N = 512, 512, 3, 512
P = 2 ** 7


def setup_inputs():
    n = np.random.standard_normal
    s = mx_kscale(K)[:, None]
    packed_xT = pack_weight(n((K, T)) * s)
    return {
        "x_words": packed_xT[0],
        "x_scales": packed_xT[1],
        "w1": (n((K, N)) / np.sqrt(K) / s).astype(np.float32),
        "gate": (np.tile(np.random.uniform(0.2, 1.0, (D, 1, T)) / np.sqrt(D), (1, P, 1))).astype(np.float32),
        "pos1": striped(np.random.permutation(T)),
        "pos2": striped(np.random.permutation(T)),
        "pos3": striped(np.random.permutation(T)),
    }


def reference(x_words, x_scales, w1, gate, pos1, pos2, pos3):
    xq = unpack_weight(x_words, x_scales)
    y = relu(mxq(f64(w1), 0, "e4m3").T @ xq)
    out_0 = y + (y[:, unstriped(pos1)] - y) * f64(gate)[0, :1] + (y[:, unstriped(pos2)] - y) * f64(gate)[1, :1] + (y[:, unstriped(pos3)] - y) * f64(gate)[2, :1]
    return (out_0,) + planes(out_0)

@@ -1,0 +1,214 @@
+from contextlib import ExitStack
+
+import concourse.mybir as mybir
+from concourse.masks import make_identity
+
+K, T, D, N = 512, 512, 3, 512
+FLOPS = 2 * K * T * N + 9 * N * T
+
+F32 = mybir.dt.float32
+BF16 = mybir.dt.bfloat16
+I32 = mybir.dt.int32
+U32 = mybir.dt.uint32
+U16 = mybir.dt.uint16
+U8 = mybir.dt.uint8
+FP8X4 = mybir.dt.float8_e4m3fn_x4
+ACT = mybir.ActivationFunctionType
+ALU = mybir.AluOpType
+
+P = 128
+PACK = 4
+VB = T // P
+HALF = T // 2
+SPARE = 8
+
+
+def tile_picked_wgrand_relu_lo_kernel(
+    tc, x_words, x_scales, w1, gate, pos1, pos2, pos3, out_0, out_1, out_2
+):
+    nc = tc.nc
+    with ExitStack() as ctx:
+        keep = ctx.enter_context(tc.tile_pool(name="keep", bufs=1))
+        ring = ctx.enter_context(tc.tile_pool(name="ring", bufs=13))
+        psum = ctx.enter_context(tc.psum_pool(name="psum", bufs=1))
+
+        xs = keep.tile([P, T], U8, name="xs", align_bytes=64)
+        nc.gpsimd.memset(xs[:].bitcast(I32), 0)
+        w_rows = w1.rearrange("(p j) m -> p j m", j=PACK)
+        w_raw = [keep.tile([P, PACK, HALF], F32, name="w_raw%d" % h) for h in range(2)]
+        nc.sync.dma_start(out=w_raw[0][:], in_=w_rows[:, :, 0:HALF])
+        xw = keep.tile([P, T], U32, name="xw", align_bytes=64)
+        nc.sync.dma_start(out=xw[:].bitcast(I32), in_=x_words[0].rearrange("p n t -> p (n t)").bitcast(I32))
+        for q in range(4):
+            nc.sync.dma_start(out=xs[32 * q : 32 * q + 4, :].bitcast(I32), in_=x_scales[0, 4 * q : 4 * q + 4, :].bitcast(I32))
+        lists = [keep.tile([P, T // 16], U16, name="list%d" % d) for d in range(D)]
+        gates = [keep.tile([P, T], F32, name="gate%d" % d) for d in range(D)]
+        nc.sync.dma_start(lists[0][:], pos1)
+        nc.sync.dma_start(out=w_raw[1][:], in_=w_rows[:, :, HALF:N])
+        nc.sync.dma_start(out=gates[0][:], in_=gate[0])
+        gate_rows = keep.tile([P, D, P], F32, name="gate_rows")
+        nc.gpsimd.memset(gate_rows[:], 0.0)
+        nc.sync.dma_start(out=gate_rows[0:VB, :, :], in_=gate[:, 0, :].rearrange("d (b c) -> b d c", b=VB))
+        nc.sync.dma_start(lists[1][:], pos2)
+        nc.sync.dma_start(out=gates[1][:], in_=gate[1])
+        nc.sync.dma_start(lists[2][:], pos3)
+        nc.sync.dma_start(out=gates[2][:], in_=gate[2])
+
+        ident = keep.tile([P, P], F32, name="ident")
+        make_identity(nc, ident[:])
+
+        ys = [keep.tile([P, T + SPARE], F32, name="y%d" % g) for g in range(4)]
+        nc.scalar.activation(ys[0][:, T:], ident[:, 0:SPARE], ACT.Relu)
+        nc.gpsimd.memset(ys[1][:, T:], 0.0)
+
+        def transpose_into(bank, src, first, last):
+            for b in range(VB):
+                nc.tensor.matmul(bank[:, b * P : (b + 1) * P], src(b), ident[:], start=first and b == 0, stop=last and b == VB - 1, is_transpose=True)
+
+        wb01 = [keep.tile([P, P * PACK], BF16, name="wb01_%d" % h, tag="wb01_%d" % h, align_bytes=64) for h in range(2)]
+        wb23 = keep.tile([P, 2 * P * PACK], BF16, name="wb23", tag="wb23", align_bytes=64)
+        wq01 = [keep.tile([P, P], U32, name="wq01_%d" % h, align_bytes=64) for h in range(2)]
+        ws01 = [keep.tile([P, P], U8, name="ws01_%d" % h, align_bytes=64) for h in range(2)]
+        wq23 = keep.tile([P, 2 * P], U32, name="wq23", align_bytes=64)
+        ws23 = keep.tile([P, 2 * P], U8, name="ws23", align_bytes=64)
+
+        def cast01(copy, h):
+            copy(out=wb01[h][:].rearrange("p (l t j) -> p l t j", t=2, j=PACK),
+                 in_=w_raw[h][:].rearrange("p j (l t) -> p l t j", t=PACK)[:, :, 0:2, :])
+
+        def cast23(copy, h):
+            copy(out=wb23[:].rearrange("p (t l j) -> p l t j", t=2, j=PACK)[:, 64 * h : 64 * h + 64, :, :],
+                 in_=w_raw[h][:].rearrange("p j (l t) -> p l t j", t=PACK)[:, :, 2:4, :])
+
+        def project(g, codes, scales):
+            acc = psum.tile([P, T], F32, name="acc", tag="bank", bufs=5)
+            nc.tensor.matmul_mx(out=acc[:], lhsT=codes.bitcast(FP8X4), lhsT_scale=scales, rhs=xw[:].bitcast(FP8X4), rhs_scale=xs[:], start=True, stop=True)
+            nc.scalar.activation(ys[g][:, 0:T], acc[:], ACT.Relu)
+
+        cast01(nc.vector.tensor_copy, 0)
+        nc.vector.quantize_mx(out=wq01[0][:].bitcast(FP8X4), scales=ws01[0][:], in_=wb01[0][:])
+        project(0, wq01[0][:], ws01[0][:])
+        cast23(nc.scalar.copy, 0)
+        cast01(nc.vector.tensor_copy, 1)
+        nc.vector.quantize_mx(out=wq01[1][:].bitcast(FP8X4), scales=ws01[1][:], in_=wb01[1][:])
+        cast23(nc.scalar.copy, 1)
+        nc.vector.quantize_mx(out=wq23[:].bitcast(FP8X4), scales=ws23[:], in_=wb23[:])
+
+        def gather(g, d, lo, hi):
+            prod = ring.tile([P, hi - lo], F32, name="prod", tag="prod")
+            nc.vector.tensor_tensor(prod[:], ys[g][:].indirect(lists[d][:, lo // 16 : hi // 16]), gates[d][:, lo:hi], ALU.mult)
+            return prod
+
+        own01 = keep.tile([P, VB, 2, P], F32, name="own01")
+        sum01 = keep.tile([P, VB, 2, P], F32, name="sum01")
+        own23 = [keep.tile([P, VB, P], F32, name="own%d" % t) for t in (2, 3)]
+        sum23 = [keep.tile([P, VB, P], F32, name="sum%d" % t) for t in (2, 3)]
+        stay = keep.tile([P, VB], F32, name="stay")
+
+        def make_stay():
+            bank = psum.tile([P, T], F32, name="turn", tag="bank", bufs=5)
+            for d in range(D):
+                nc.tensor.matmul(bank[:, 0:P], gate_rows[:, d, :], ident[:], start=d == 0, stop=d == D - 1, is_transpose=True)
+            nc.scalar.activation(stay[:], bank[:, 0:VB], ACT.Copy, bias=1.0, scale=-1.0)
+
+        def own_term(g):
+            bank = psum.tile([P, T], F32, name="turn", tag="bank", bufs=5)
+            transpose_into(bank, lambda b: ys[g][:, b * P : (b + 1) * P], True, True)
+            for b in range(VB):
+                src = bank[:, b * P : (b + 1) * P]
+                if g < 2:
+                    nc.scalar.activation(own01[:, b, :, 64 * g : 64 * g + 64], src.rearrange("p (l t) -> p t l", t=2), ACT.Copy, scale=stay[:, b : b + 1])
+                else:
+                    nc.scalar.activation(own23[g - 2][:, b, :], src, ACT.Copy, scale=stay[:, b : b + 1])
+
+        banks = {}
+
+        def neighbour(g, d, last):
+            if d == 0:
+                banks[g] = psum.tile([P, T], F32, name="sums", tag="sums", bufs=3)
+            prod = gather(g, d, 0, T)
+            transpose_into(banks[g], lambda b: prod[:, b * P : (b + 1) * P], d == 0, last)
+
+        def empty_sums(g):
+            if g < 2:
+                nc.scalar.copy(sum01[:, :, :, 64 * g : 64 * g + 64], banks[g][:].rearrange("p (b l t) -> p b t l", b=VB, t=2))
+            else:
+                nc.scalar.copy(sum23[g - 2][:].rearrange("p b l -> p (b l)"), banks[g][:])
+
+        res = [keep.tile([P, PACK, HALF], F32, name="res%d" % h) for h in range(2)]
+        out_rows = out_0.rearrange("(l t) v -> l t v", t=PACK)
+
+        def back_own(t):
+            bank = psum.tile([P, T], F32, name="back", tag="bank", bufs=5)
+            transpose_into(bank, lambda b: own01[:, b, t, :] if t < 2 else own23[t - 2][:, b, :], True, False)
+            return bank
+
+        def back_sum(bank, t):
+            transpose_into(bank, lambda b: sum01[:, b, t, :] if t < 2 else sum23[t - 2][:, b, :], False, True)
+
+        def finish(bank, t):
+            for h in range(2):
+                nc.scalar.copy(res[h][:, t, :], bank[:, h * HALF : (h + 1) * HALF])
+
+        def store(t0, t1, h):
+            nc.sync.dma_start(out=out_rows[:, t0:t1, h * HALF : (h + 1) * HALF], in_=res[h][:, t0:t1, :])
+
+        project(1, wq01[1][:], ws01[1][:])
+        make_stay()
+        own_term(0)
+        neighbour(0, 0, False)
+        project(2, wq23[:, 0:P], ws23[:, 0:P])
+        own_term(1)
+        neighbour(0, 1, False)
+        project(3, wq23[:, P : 2 * P], ws23[:, P : 2 * P])
+        nc.scalar.copy(ys[2][:, T:], ys[3][:, 0:SPARE])
+        nc.scalar.copy(ys[3][:, T:], ys[2][:, T:])
+        own_term(2)
+        neighbour(0, 2, True)
+        own_term(3)
+        empty_sums(0)
+        back0 = back_own(0)
+        neighbour(1, 0, False)
+        back1 = back_own(1)
+        neighbour(1, 1, False)
+        back2 = back_own(2)
+        back3 = back_own(3)
+        neighbour(1, 2, True)
+        empty_sums(1)
+        neighbour(2, 0, False)
+        back_sum(back0, 0)
+        finish(back0, 0)
+        neighbour(3, 0, False)
+        back_sum(back1, 1)
+        finish(back1, 1)
+        for h in range(2):
+            store(0, 2, h)
+        neighbour(2, 1, True)
+        empty_sums(2)
+        neighbour(3, 1, True)
+        empty_sums(3)
+        back_sum(back2, 2)
+        back_sum(back3, 3)
+
+        last2 = gather(2, 2, 0, T)
+        last3 = [gather(3, 2, 0, HALF)]
+        nc.vector.tensor_tensor(res[0][:, 2, :], back2[:, 0:HALF], last2[:, 0:HALF], ALU.add)
+        nc.vector.tensor_tensor(res[1][:, 2, :], back2[:, HALF:T], last2[:, HALF:T], ALU.add)
+        nc.vector.tensor_tensor(res[0][:, 3, :], back3[:, 0:HALF], last3[0][:], ALU.add)
+        store(2, 4, 0)
+        last3.append(gather(3, 2, HALF, T))
+        nc.vector.tensor_tensor(res[1][:, 3, :], back3[:, HALF:T], last3[1][:], ALU.add)
+        store(2, 4, 1)
+        rounded = [keep.tile([P, HALF * PACK], BF16, name="rounded%d" % h, align_bytes=64) for h in range(2)]
+        codes = keep.tile([P, T], U32, name="codes", align_bytes=64)
+        scales = keep.tile([P, T], U8, name="scales", align_bytes=64)
+        for h, copy in enumerate((nc.scalar.copy, nc.vector.tensor_copy)):
+            copy(out=rounded[h][:].rearrange("p (c i t) -> p c t i", i=4, t=PACK), in_=res[h][:].rearrange("p t (c i) -> p c t i", i=4))
+        words_out = out_1[0].rearrange("p n t -> p (n t)").bitcast(I32)
+        for h in range(2):
+            cols = slice(h * HALF, (h + 1) * HALF)
+            nc.vector.quantize_mx(out=codes[:, cols].bitcast(FP8X4), scales=scales[:, cols], in_=rounded[h][:])
+            nc.sync.dma_start(out=words_out[:, cols], in_=codes[:, cols].bitcast(I32))
+        for q in range(4):
+            queue = nc.scalar if q % 2 == 0 else nc.sync
+            queue.dma_start(out=out_2[0, 4 * q : 4 * q + 4, :].bitcast(I32), in_=scales[32 * q : 32 * q + 4, :].bitcast(I32))

@@ -38,9 +38,9 @@ def tile_picked_wgrand_relu_lo_kernel(
         w_raw = [keep.tile([P, PACK, HALF], F32, name="w_raw%d" % h) for h in range(2)]
         nc.sync.dma_start(out=w_raw[0][:], in_=w_rows[:, :, 0:HALF])
         xw = keep.tile([P, T], U32, name="xw", align_bytes=64)
-        nc.sync.dma_start(out=xw[:].bitcast(I32), in_=x_words[0].rearrange("p n t -> p (n t)").bitcast(I32))
         for q in range(4):
             nc.sync.dma_start(out=xs[32 * q : 32 * q + 4, :].bitcast(I32), in_=x_scales[0, 4 * q : 4 * q + 4, :].bitcast(I32))
+        nc.sync.dma_start(out=xw[:].bitcast(I32), in_=x_words[0].rearrange("p n t -> p (n t)").bitcast(I32))
         lists = [keep.tile([P, T // 16], U16, name="list%d" % d) for d in range(D)]
         gates = [keep.tile([P, T], F32, name="gate%d" % d) for d in range(D)]
         nc.sync.dma_start(lists[0][:], pos1)
@@ -65,39 +65,45 @@ def tile_picked_wgrand_relu_lo_kernel(
             for b in range(VB):
                 nc.tensor.matmul(bank[:, b * P : (b + 1) * P], src(b), ident[:], start=first and b == 0, stop=last and b == VB - 1, is_transpose=True)
 
-        wb01 = [keep.tile([P, P * PACK], BF16, name="wb01_%d" % h, tag="wb01_%d" % h, align_bytes=64) for h in range(2)]
-        wb23 = keep.tile([P, 2 * P * PACK], BF16, name="wb23", tag="wb23", align_bytes=64)
-        wq01 = [keep.tile([P, P], U32, name="wq01_%d" % h, align_bytes=64) for h in range(2)]
-        ws01 = [keep.tile([P, P], U8, name="ws01_%d" % h, align_bytes=64) for h in range(2)]
-        wq23 = keep.tile([P, 2 * P], U32, name="wq23", align_bytes=64)
-        ws23 = keep.tile([P, 2 * P], U8, name="ws23", align_bytes=64)
+        wb0 = keep.tile([P, P * PACK], BF16, name="wb0", align_bytes=64)
+        wq0 = keep.tile([P, P], U32, name="wq0", align_bytes=64)
+        ws0 = keep.tile([P, P], U8, name="ws0", align_bytes=64)
+        wb = keep.tile([P, 3 * P * PACK], BF16, name="wb", align_bytes=64)
+        wq = keep.tile([P, 3 * P], U32, name="wq", align_bytes=64)
+        ws = keep.tile([P, 3 * P], U8, name="ws", align_bytes=64)
+        w_cols = [w_raw[h][:].rearrange("p j (l t) -> p l t j", t=PACK) for h in range(2)]
 
-        def cast01(copy, h):
-            copy(out=wb01[h][:].rearrange("p (l t j) -> p l t j", t=2, j=PACK),
-                 in_=w_raw[h][:].rearrange("p j (l t) -> p l t j", t=PACK)[:, :, 0:2, :])
+        def cast01(copy, dst, h, lo, hi):
+            copy(out=dst.rearrange("p (l t j) -> p l t j", t=2, j=PACK)[:, lo:hi, :, :], in_=w_cols[h][:, lo:hi, 0:2, :])
 
         def cast23(copy, h):
-            copy(out=wb23[:].rearrange("p (t l j) -> p l t j", t=2, j=PACK)[:, 64 * h : 64 * h + 64, :, :],
-                 in_=w_raw[h][:].rearrange("p j (l t) -> p l t j", t=PACK)[:, :, 2:4, :])
+            copy(out=wb[:, P * PACK :].rearrange("p (t l j) -> p l t j", t=2, j=PACK)[:, 64 * h : 64 * h + 64, :, :], in_=w_cols[h][:, :, 2:4, :])
 
-        def project(g, codes, scales):
-            acc = psum.tile([P, T], F32, name="acc", tag="bank", bufs=5)
-            nc.tensor.matmul_mx(out=acc[:], lhsT=codes.bitcast(FP8X4), lhsT_scale=scales, rhs=xw[:].bitcast(FP8X4), rhs_scale=xs[:], start=True, stop=True)
-            nc.scalar.activation(ys[g][:, 0:T], acc[:], ACT.Relu)
+        def new_bank(name):
+            return psum.tile([P, T], F32, name=name, tag="bank", bufs=5)
 
-        cast01(nc.vector.tensor_copy, 0)
-        nc.vector.quantize_mx(out=wq01[0][:].bitcast(FP8X4), scales=ws01[0][:], in_=wb01[0][:])
-        project(0, wq01[0][:], ws01[0][:])
-        cast23(nc.scalar.copy, 0)
-        cast01(nc.vector.tensor_copy, 1)
-        nc.vector.quantize_mx(out=wq01[1][:].bitcast(FP8X4), scales=ws01[1][:], in_=wb01[1][:])
+        def project(g, codes, scales, lo, hi):
+            acc = new_bank("acc")
+            nc.tensor.matmul_mx(out=acc[:, 0 : hi - lo], lhsT=codes.bitcast(FP8X4), lhsT_scale=scales, rhs=xw[:, lo:hi].bitcast(FP8X4), rhs_scale=xs[:, lo:hi], start=True, stop=True)
+            nc.scalar.activation(ys[g][:, lo:hi], acc[:, 0 : hi - lo], ACT.Relu)
+
+        cast01(nc.vector.tensor_copy, wb0[:], 0, 0, 40)
+        cast01(nc.scalar.copy, wb0[:], 0, 40, 64)
+        nc.vector.quantize_mx(out=wq0[:].bitcast(FP8X4), scales=ws0[:], in_=wb0[:])
+        project(0, wq0[:], ws0[:], 0, HALF)
+        project(0, wq0[:], ws0[:], HALF, T)
+        cast23(nc.vector.tensor_copy, 0)
+        cast01(nc.vector.tensor_copy, wb[:, 0 : P * PACK], 1, 0, 64)
         cast23(nc.scalar.copy, 1)
-        nc.vector.quantize_mx(out=wq23[:].bitcast(FP8X4), scales=ws23[:], in_=wb23[:])
+        nc.vector.quantize_mx(out=wq[:, 0 : 2 * P].bitcast(FP8X4), scales=ws[:, 0 : 2 * P], in_=wb[:, 0 : 2 * P * PACK])
+        nc.vector.quantize_mx(out=wq[:, 2 * P :].bitcast(FP8X4), scales=ws[:, 2 * P :], in_=wb[:, 2 * P * PACK :])
+        for g in range(1, 4):
+            project(g, wq[:, (g - 1) * P : g * P], ws[:, (g - 1) * P : g * P], 0, T)
+        nc.scalar.copy(ys[2][:, T:], ys[3][:, 0:SPARE])
+        nc.scalar.copy(ys[3][:, T:], ys[2][:, T:])
 
-        def gather(g, d, lo, hi):
-            prod = ring.tile([P, hi - lo], F32, name="prod", tag="prod")
-            nc.vector.tensor_tensor(prod[:], ys[g][:].indirect(lists[d][:, lo // 16 : hi // 16]), gates[d][:, lo:hi], ALU.mult)
-            return prod
+        def gather(prod, g, d, lo, hi):
+            nc.vector.tensor_tensor(prod, ys[g][:].indirect(lists[d][:, lo // 16 : hi // 16]), gates[d][:, lo:hi], ALU.mult)
 
         own01 = keep.tile([P, VB, 2, P], F32, name="own01")
         sum01 = keep.tile([P, VB, 2, P], F32, name="sum01")
@@ -106,13 +112,13 @@ def tile_picked_wgrand_relu_lo_kernel(
         stay = keep.tile([P, VB], F32, name="stay")
 
         def make_stay():
-            bank = psum.tile([P, T], F32, name="turn", tag="bank", bufs=5)
+            bank = new_bank("turn")
             for d in range(D):
                 nc.tensor.matmul(bank[:, 0:P], gate_rows[:, d, :], ident[:], start=d == 0, stop=d == D - 1, is_transpose=True)
             nc.scalar.activation(stay[:], bank[:, 0:VB], ACT.Copy, bias=1.0, scale=-1.0)
 
         def own_term(g):
-            bank = psum.tile([P, T], F32, name="turn", tag="bank", bufs=5)
+            bank = new_bank("turn")
             transpose_into(bank, lambda b: ys[g][:, b * P : (b + 1) * P], True, True)
             for b in range(VB):
                 src = bank[:, b * P : (b + 1) * P]
@@ -126,84 +132,90 @@ def tile_picked_wgrand_relu_lo_kernel(
         def neighbour(g, d, last):
             if d == 0:
                 banks[g] = psum.tile([P, T], F32, name="sums", tag="sums", bufs=3)
-            prod = gather(g, d, 0, T)
+            prod = ring.tile([P, T], F32, name="prod", tag="prod")
+            gather(prod[:], g, d, 0, T)
             transpose_into(banks[g], lambda b: prod[:, b * P : (b + 1) * P], d == 0, last)
 
         def empty_sums(g):
             if g < 2:
                 nc.scalar.copy(sum01[:, :, :, 64 * g : 64 * g + 64], banks[g][:].rearrange("p (b l t) -> p b t l", b=VB, t=2))
             else:
-                nc.scalar.copy(sum23[g - 2][:].rearrange("p b l -> p (b l)"), banks[g][:])
+                for h in range(2):
+                    nc.scalar.copy(sum23[g - 2][:, 2 * h : 2 * h + 2, :].rearrange("p b l -> p (b l)"), banks[g][:, h * HALF : (h + 1) * HALF])
 
-        res = [keep.tile([P, PACK, HALF], F32, name="res%d" % h) for h in range(2)]
+        res = [[keep.tile([P, 2, HALF], F32, name="res%d%d" % (pair, h)) for h in range(2)] for pair in range(2)]
         out_rows = out_0.rearrange("(l t) v -> l t v", t=PACK)
 
-        def back_own(t):
-            bank = psum.tile([P, T], F32, name="back", tag="bank", bufs=5)
-            transpose_into(bank, lambda b: own01[:, b, t, :] if t < 2 else own23[t - 2][:, b, :], True, False)
+        def turn_back(bank, pair, h, src01, src23, first):
+            for i in range(4):
+                t, b = 2 * pair + i // 2, 2 * h + i % 2
+                src = src01[:, b, t, :] if pair == 0 else src23[t - 2][:, b, :]
+                nc.tensor.matmul(bank[:, i * P : (i + 1) * P], src, ident[:], start=first and i == 0, stop=not first and i == 3, is_transpose=True)
+
+        def back_own(pair, h):
+            bank = new_bank("back")
+            turn_back(bank, pair, h, own01, own23, True)
             return bank
 
-        def back_sum(bank, t):
-            transpose_into(bank, lambda b: sum01[:, b, t, :] if t < 2 else sum23[t - 2][:, b, :], False, True)
+        def back_sum(bank, pair, h):
+            turn_back(bank, pair, h, sum01, sum23, False)
 
-        def finish(bank, t):
-            for h in range(2):
-                nc.scalar.copy(res[h][:, t, :], bank[:, h * HALF : (h + 1) * HALF])
+        def store(pair, h):
+            nc.sync.dma_start(out=out_rows[:, 2 * pair : 2 * pair + 2, h * HALF : (h + 1) * HALF], in_=res[pair][h][:])
 
-        def store(t0, t1, h):
-            nc.sync.dma_start(out=out_rows[:, t0:t1, h * HALF : (h + 1) * HALF], in_=res[h][:, t0:t1, :])
+        rounded = [keep.tile([P, HALF * PACK], BF16, name="rounded%d" % h, align_bytes=64) for h in range(2)]
 
-        project(1, wq01[1][:], ws01[1][:])
+        def round_pair(copy, pair, h):
+            copy(out=rounded[h][:].rearrange("p (c t) -> p c t", t=PACK)[:, :, 2 * pair : 2 * pair + 2], in_=res[pair][h][:].rearrange("p t c -> p c t"))
+
+        def finish(bank, h):
+            nc.scalar.copy(res[0][h][:].rearrange("p t c -> p (t c)"), bank[:])
+            store(0, h)
+
         make_stay()
         own_term(0)
         neighbour(0, 0, False)
-        project(2, wq23[:, 0:P], ws23[:, 0:P])
         own_term(1)
         neighbour(0, 1, False)
-        project(3, wq23[:, P : 2 * P], ws23[:, P : 2 * P])
-        nc.scalar.copy(ys[2][:, T:], ys[3][:, 0:SPARE])
-        nc.scalar.copy(ys[3][:, T:], ys[2][:, T:])
         own_term(2)
-        neighbour(0, 2, True)
         own_term(3)
+        neighbour(0, 2, True)
         empty_sums(0)
-        back0 = back_own(0)
+        back = {}
+        back[0, 0] = back_own(0, 0)
         neighbour(1, 0, False)
-        back1 = back_own(1)
+        back[0, 1] = back_own(0, 1)
         neighbour(1, 1, False)
-        back2 = back_own(2)
-        back3 = back_own(3)
+        back[1, 0] = back_own(1, 0)
         neighbour(1, 2, True)
         empty_sums(1)
+        back[1, 1] = back_own(1, 1)
         neighbour(2, 0, False)
-        back_sum(back0, 0)
-        finish(back0, 0)
+        back_sum(back[0, 0], 0, 0)
+        finish(back[0, 0], 0)
         neighbour(3, 0, False)
-        back_sum(back1, 1)
-        finish(back1, 1)
-        for h in range(2):
-            store(0, 2, h)
+        back_sum(back[0, 1], 0, 1)
+        finish(back[0, 1], 1)
         neighbour(2, 1, True)
         empty_sums(2)
         neighbour(3, 1, True)
         empty_sums(3)
-        back_sum(back2, 2)
-        back_sum(back3, 3)
+        for h in range(2):
+            back_sum(back[1, h], 1, h)
+        for h in range(2):
+            round_pair(nc.scalar.copy, 0, h)
 
-        last2 = gather(2, 2, 0, T)
-        last3 = [gather(3, 2, 0, HALF)]
-        nc.vector.tensor_tensor(res[0][:, 2, :], back2[:, 0:HALF], last2[:, 0:HALF], ALU.add)
-        nc.vector.tensor_tensor(res[1][:, 2, :], back2[:, HALF:T], last2[:, HALF:T], ALU.add)
-        nc.vector.tensor_tensor(res[0][:, 3, :], back3[:, 0:HALF], last3[0][:], ALU.add)
-        store(2, 4, 0)
-        last3.append(gather(3, 2, HALF, T))
-        nc.vector.tensor_tensor(res[1][:, 3, :], back3[:, HALF:T], last3[1][:], ALU.add)
-        store(2, 4, 1)
-        rounded = [keep.tile([P, HALF * PACK], BF16, name="rounded%d" % h, align_bytes=64) for h in range(2)]
+        last = [keep.tile([P, 2, HALF], F32, name="last%d" % h) for h in range(2)]
+        for h in range(2):
+            for g in (2, 3):
+                gather(last[h][:, g - 2, :], g, 2, h * HALF, (h + 1) * HALF)
+        for h in range(2):
+            nc.vector.tensor_tensor(res[1][h][:].rearrange("p t c -> p (t c)"), back[1, h][:], last[h][:].rearrange("p t c -> p (t c)"), ALU.add)
+            store(1, h)
+        round_pair(nc.scalar.copy, 1, 0)
+        round_pair(nc.vector.tensor_copy, 1, 1)
         codes = keep.tile([P, T], U32, name="codes", align_bytes=64)
         scales = keep.tile([P, T], U8, name="scales", align_bytes=64)
-        for h, copy in enumerate((nc.scalar.copy, nc.vector.tensor_copy)):
-            copy(out=rounded[h][:].rearrange("p (c i t) -> p c t i", i=4, t=PACK), in_=res[h][:].rearrange("p t (c i) -> p c t i", i=4))
         words_out = out_1[0].rearrange("p n t -> p (n t)").bitcast(I32)
         for h in range(2):
             cols = slice(h * HALF, (h + 1) * HALF)

@@ -40,15 +40,15 @@ def tile_picked_wgrand_relu_lo_kernel(
         xw = keep.tile([P, T], U32, name="xw", align_bytes=64)
         for q in range(4):
             nc.sync.dma_start(out=xs[32 * q : 32 * q + 4, :].bitcast(I32), in_=x_scales[0, 4 * q : 4 * q + 4, :].bitcast(I32))
-        nc.sync.dma_start(out=xw[:].bitcast(I32), in_=x_words[0].rearrange("p n t -> p (n t)").bitcast(I32))
-        lists = [keep.tile([P, T // 16], U16, name="list%d" % d) for d in range(D)]
-        gates = [keep.tile([P, T], F32, name="gate%d" % d) for d in range(D)]
-        nc.sync.dma_start(lists[0][:], pos1)
-        nc.sync.dma_start(out=w_raw[1][:], in_=w_rows[:, :, HALF:N])
-        nc.sync.dma_start(out=gates[0][:], in_=gate[0])
         gate_rows = keep.tile([P, D, P], F32, name="gate_rows")
         nc.gpsimd.memset(gate_rows[:], 0.0)
         nc.sync.dma_start(out=gate_rows[0:VB, :, :], in_=gate[:, 0, :].rearrange("d (b c) -> b d c", b=VB))
+        nc.sync.dma_start(out=xw[:].bitcast(I32), in_=x_words[0].rearrange("p n t -> p (n t)").bitcast(I32))
+        lists = [keep.tile([P, T // 16], U16, name="list%d" % d) for d in range(D)]
+        gates = [keep.tile([P, T], F32, name="gate%d" % d) for d in range(D)]
+        nc.sync.dma_start(out=w_raw[1][:], in_=w_rows[:, :, HALF:N])
+        nc.sync.dma_start(lists[0][:], pos1)
+        nc.sync.dma_start(out=gates[0][:], in_=gate[0])
         nc.sync.dma_start(lists[1][:], pos2)
         nc.sync.dma_start(out=gates[1][:], in_=gate[1])
         nc.sync.dma_start(lists[2][:], pos3)
@@ -92,15 +92,19 @@ def tile_picked_wgrand_relu_lo_kernel(
         nc.vector.quantize_mx(out=wq0[:].bitcast(FP8X4), scales=ws0[:], in_=wb0[:])
         project(0, wq0[:], ws0[:], 0, HALF)
         project(0, wq0[:], ws0[:], HALF, T)
-        cast23(nc.vector.tensor_copy, 0)
+        warm = new_bank("warm")
+        nc.tensor.matmul_mx(out=warm[:], lhsT=wq0[:].bitcast(FP8X4), lhsT_scale=ws0[:], rhs=xw[:].bitcast(FP8X4), rhs_scale=xs[:], start=True, stop=True)
+        cast23(nc.scalar.copy, 0)
         cast01(nc.vector.tensor_copy, wb[:, 0 : P * PACK], 1, 0, 64)
-        cast23(nc.scalar.copy, 1)
-        nc.vector.quantize_mx(out=wq[:, 0 : 2 * P].bitcast(FP8X4), scales=ws[:, 0 : 2 * P], in_=wb[:, 0 : 2 * P * PACK])
-        nc.vector.quantize_mx(out=wq[:, 2 * P :].bitcast(FP8X4), scales=ws[:, 2 * P :], in_=wb[:, 2 * P * PACK :])
-        for g in range(1, 4):
-            project(g, wq[:, (g - 1) * P : g * P], ws[:, (g - 1) * P : g * P], 0, T)
-        nc.scalar.copy(ys[2][:, T:], ys[3][:, 0:SPARE])
-        nc.scalar.copy(ys[3][:, T:], ys[2][:, T:])
+        cast23(nc.vector.tensor_copy, 1)
+        nc.vector.quantize_mx(out=wq[:, 0:P].bitcast(FP8X4), scales=ws[:, 0:P], in_=wb[:, 0 : P * PACK])
+        nc.vector.quantize_mx(out=wq[:, P:].bitcast(FP8X4), scales=ws[:, P:], in_=wb[:, P * PACK :])
+
+        def project_rest():
+            for g in range(1, 4):
+                project(g, wq[:, (g - 1) * P : g * P], ws[:, (g - 1) * P : g * P], 0, T)
+            nc.scalar.copy(ys[2][:, T:], ys[3][:, 0:SPARE])
+            nc.scalar.copy(ys[3][:, T:], ys[2][:, T:])
 
         def gather(prod, g, d, lo, hi):
             nc.vector.tensor_tensor(prod, ys[g][:].indirect(lists[d][:, lo // 16 : hi // 16]), gates[d][:, lo:hi], ALU.mult)
@@ -173,37 +177,38 @@ def tile_picked_wgrand_relu_lo_kernel(
             store(0, h)
 
         make_stay()
+        back = {}
         own_term(0)
-        neighbour(0, 0, False)
+        project_rest()
         own_term(1)
-        neighbour(0, 1, False)
+        neighbour(0, 0, False)
         own_term(2)
-        own_term(3)
+        neighbour(0, 1, False)
         neighbour(0, 2, True)
         empty_sums(0)
-        back = {}
         back[0, 0] = back_own(0, 0)
-        neighbour(1, 0, False)
         back[0, 1] = back_own(0, 1)
+        neighbour(1, 0, False)
         neighbour(1, 1, False)
-        back[1, 0] = back_own(1, 0)
         neighbour(1, 2, True)
         empty_sums(1)
-        back[1, 1] = back_own(1, 1)
-        neighbour(2, 0, False)
+        own_term(3)
         back_sum(back[0, 0], 0, 0)
         finish(back[0, 0], 0)
-        neighbour(3, 0, False)
         back_sum(back[0, 1], 0, 1)
         finish(back[0, 1], 1)
+        round_pair(nc.scalar.copy, 0, 0)
+        round_pair(nc.scalar.copy, 0, 1)
+        neighbour(2, 0, False)
+        back[1, 0] = back_own(1, 0)
+        neighbour(3, 0, False)
+        back[1, 1] = back_own(1, 1)
         neighbour(2, 1, True)
         empty_sums(2)
         neighbour(3, 1, True)
         empty_sums(3)
-        for h in range(2):
-            back_sum(back[1, h], 1, h)
-        for h in range(2):
-            round_pair(nc.scalar.copy, 0, h)
+        back_sum(back[1, 0], 1, 0)
+        back_sum(back[1, 1], 1, 1)
 
         last = [keep.tile([P, 2, HALF], F32, name="last%d" % h) for h in range(2)]
         for h in range(2):

@@ -18,9 +18,17 @@ ALU = mybir.AluOpType
 
 P = 128
 PACK = 4
-VB = T // P
+PAIR = 2
+QUADRANTS = 4
+BLOCKS = T // P
 HALF = T // 2
+L_HALF = P // 2
+PER_COLUMN = 16
 SPARE = 8
+L_VECTOR = 40
+TRANSPOSED_TERMS = 10
+SUM_BANKS = 3
+OTHER_BANKS = 5
 
 
 def tile_picked_wgrand_relu_lo_kernel(
@@ -29,30 +37,29 @@ def tile_picked_wgrand_relu_lo_kernel(
     nc = tc.nc
     with ExitStack() as ctx:
         keep = ctx.enter_context(tc.tile_pool(name="keep", bufs=1))
-        ring = ctx.enter_context(tc.tile_pool(name="ring", bufs=13))
+        ring = ctx.enter_context(tc.tile_pool(name="ring", bufs=TRANSPOSED_TERMS))
         psum = ctx.enter_context(tc.psum_pool(name="psum", bufs=1))
 
-        xs = keep.tile([P, T], U8, name="xs", align_bytes=64)
-        nc.gpsimd.memset(xs[:].bitcast(I32), 0)
+        x_scale = keep.tile([P, T], U8, name="x_scale", align_bytes=64)
+        nc.gpsimd.memset(x_scale[:].bitcast(I32), 0)
         w_rows = w1.rearrange("(p j) m -> p j m", j=PACK)
         w_raw = [keep.tile([P, PACK, HALF], F32, name="w_raw%d" % h) for h in range(2)]
         nc.sync.dma_start(out=w_raw[0][:], in_=w_rows[:, :, 0:HALF])
-        xw = keep.tile([P, T], U32, name="xw", align_bytes=64)
-        for q in range(4):
-            nc.sync.dma_start(out=xs[32 * q : 32 * q + 4, :].bitcast(I32), in_=x_scales[0, 4 * q : 4 * q + 4, :].bitcast(I32))
+        x_codes = keep.tile([P, T], U32, name="x_codes", align_bytes=64)
+        for q in range(QUADRANTS):
+            nc.sync.dma_start(
+                out=x_scale[32 * q : 32 * q + 4, :].bitcast(I32), in_=x_scales[0, 4 * q : 4 * q + 4, :].bitcast(I32)
+            )
         gate_rows = keep.tile([P, D, P], F32, name="gate_rows")
         nc.gpsimd.memset(gate_rows[:], 0.0)
-        nc.sync.dma_start(out=gate_rows[0:VB, :, :], in_=gate[:, 0, :].rearrange("d (b c) -> b d c", b=VB))
-        nc.sync.dma_start(out=xw[:].bitcast(I32), in_=x_words[0].rearrange("p n t -> p (n t)").bitcast(I32))
-        lists = [keep.tile([P, T // 16], U16, name="list%d" % d) for d in range(D)]
+        nc.sync.dma_start(out=gate_rows[0:BLOCKS, :, :], in_=gate[:, 0, :].rearrange("d (b c) -> b d c", b=BLOCKS))
+        nc.sync.dma_start(out=x_codes[:].bitcast(I32), in_=x_words[0].rearrange("p n t -> p (n t)").bitcast(I32))
+        lists = [keep.tile([P, T // PER_COLUMN], U16, name="list%d" % d) for d in range(D)]
         gates = [keep.tile([P, T], F32, name="gate%d" % d) for d in range(D)]
         nc.sync.dma_start(out=w_raw[1][:], in_=w_rows[:, :, HALF:N])
-        nc.sync.dma_start(lists[0][:], pos1)
-        nc.sync.dma_start(out=gates[0][:], in_=gate[0])
-        nc.sync.dma_start(lists[1][:], pos2)
-        nc.sync.dma_start(out=gates[1][:], in_=gate[1])
-        nc.sync.dma_start(lists[2][:], pos3)
-        nc.sync.dma_start(out=gates[2][:], in_=gate[2])
+        for d, pos in enumerate((pos1, pos2, pos3)):
+            nc.sync.dma_start(lists[d][:], pos)
+            nc.sync.dma_start(out=gates[d][:], in_=gate[d])
 
         ident = keep.tile([P, P], F32, name="ident")
         make_identity(nc, ident[:])
@@ -61,171 +68,202 @@ def tile_picked_wgrand_relu_lo_kernel(
         nc.scalar.activation(ys[0][:, T:], ident[:, 0:SPARE], ACT.Relu)
         nc.gpsimd.memset(ys[1][:, T:], 0.0)
 
-        def transpose_into(bank, src, first, last):
-            for b in range(VB):
-                nc.tensor.matmul(bank[:, b * P : (b + 1) * P], src(b), ident[:], start=first and b == 0, stop=last and b == VB - 1, is_transpose=True)
+        def new_bank(name):
+            return psum.tile([P, T], F32, name=name, tag="bank", bufs=OTHER_BANKS)
 
-        wb0 = keep.tile([P, P * PACK], BF16, name="wb0", align_bytes=64)
-        wq0 = keep.tile([P, P], U32, name="wq0", align_bytes=64)
-        ws0 = keep.tile([P, P], U8, name="ws0", align_bytes=64)
-        wb = keep.tile([P, 3 * P * PACK], BF16, name="wb", align_bytes=64)
-        wq = keep.tile([P, 3 * P], U32, name="wq", align_bytes=64)
-        ws = keep.tile([P, 3 * P], U8, name="ws", align_bytes=64)
+        def transpose(dst, src, start, stop):
+            nc.tensor.matmul(dst, src, ident[:], start=start, stop=stop, is_transpose=True)
+
+        def transpose_blocks(bank, src, first, last):
+            for b in range(BLOCKS):
+                cols = slice(b * P, (b + 1) * P)
+                transpose(bank[:, cols], src[:, cols], first and b == 0, last and b == BLOCKS - 1)
+
+        first_bf16 = keep.tile([P, P * PACK], BF16, name="first_bf16", align_bytes=64)
+        first_codes = keep.tile([P, P], U32, name="first_codes", align_bytes=64)
+        first_scale = keep.tile([P, P], U8, name="first_scale", align_bytes=64)
+        rest_bf16 = keep.tile([P, 3 * P * PACK], BF16, name="rest_bf16", align_bytes=64)
+        rest_codes = keep.tile([P, 3 * P], U32, name="rest_codes", align_bytes=64)
+        rest_scale = keep.tile([P, 3 * P], U8, name="rest_scale", align_bytes=64)
         w_cols = [w_raw[h][:].rearrange("p j (l t) -> p l t j", t=PACK) for h in range(2)]
 
-        def cast01(copy, dst, h, lo, hi):
-            copy(out=dst.rearrange("p (l t j) -> p l t j", t=2, j=PACK)[:, lo:hi, :, :], in_=w_cols[h][:, lo:hi, 0:2, :])
+        def round_w_pair0(copy, dst, h, lo, hi):
+            copy(
+                out=dst.rearrange("p (l t j) -> p l t j", t=PAIR, j=PACK)[:, lo:hi, :, :],
+                in_=w_cols[h][:, lo:hi, 0:PAIR, :],
+            )
 
-        def cast23(copy, h):
-            copy(out=wb[:, P * PACK :].rearrange("p (t l j) -> p l t j", t=2, j=PACK)[:, 64 * h : 64 * h + 64, :, :], in_=w_cols[h][:, :, 2:4, :])
+        def round_w_pair1(copy, h):
+            dst = rest_bf16[:, P * PACK :].rearrange("p (t l j) -> p l t j", t=PAIR, j=PACK)
+            copy(out=dst[:, L_HALF * h : L_HALF * (h + 1), :, :], in_=w_cols[h][:, :, PAIR:PACK, :])
 
-        def new_bank(name):
-            return psum.tile([P, T], F32, name=name, tag="bank", bufs=5)
-
-        def project(g, codes, scales, lo, hi):
+        def project(g, w_codes, w_scale, lo, hi):
             acc = new_bank("acc")
-            nc.tensor.matmul_mx(out=acc[:, 0 : hi - lo], lhsT=codes.bitcast(FP8X4), lhsT_scale=scales, rhs=xw[:, lo:hi].bitcast(FP8X4), rhs_scale=xs[:, lo:hi], start=True, stop=True)
+            nc.tensor.matmul_mx(
+                out=acc[:, 0 : hi - lo],
+                lhsT=w_codes.bitcast(FP8X4),
+                lhsT_scale=w_scale,
+                rhs=x_codes[:, lo:hi].bitcast(FP8X4),
+                rhs_scale=x_scale[:, lo:hi],
+                start=True,
+                stop=True,
+            )
             nc.scalar.activation(ys[g][:, lo:hi], acc[:, 0 : hi - lo], ACT.Relu)
 
-        cast01(nc.vector.tensor_copy, wb0[:], 0, 0, 40)
-        cast01(nc.scalar.copy, wb0[:], 0, 40, 64)
-        nc.vector.quantize_mx(out=wq0[:].bitcast(FP8X4), scales=ws0[:], in_=wb0[:])
-        project(0, wq0[:], ws0[:], 0, HALF)
-        project(0, wq0[:], ws0[:], HALF, T)
-        warm = new_bank("warm")
-        nc.tensor.matmul_mx(out=warm[:], lhsT=wq0[:].bitcast(FP8X4), lhsT_scale=ws0[:], rhs=xw[:].bitcast(FP8X4), rhs_scale=xs[:], start=True, stop=True)
-        cast23(nc.scalar.copy, 0)
-        cast01(nc.vector.tensor_copy, wb[:, 0 : P * PACK], 1, 0, 64)
-        cast23(nc.vector.tensor_copy, 1)
-        nc.vector.quantize_mx(out=wq[:, 0:P].bitcast(FP8X4), scales=ws[:, 0:P], in_=wb[:, 0 : P * PACK])
-        nc.vector.quantize_mx(out=wq[:, P:].bitcast(FP8X4), scales=ws[:, P:], in_=wb[:, P * PACK :])
+        round_w_pair0(nc.vector.tensor_copy, first_bf16[:], 0, 0, L_VECTOR)
+        round_w_pair0(nc.scalar.copy, first_bf16[:], 0, L_VECTOR, L_HALF)
+        nc.vector.quantize_mx(out=first_codes[:].bitcast(FP8X4), scales=first_scale[:], in_=first_bf16[:])
+        project(0, first_codes[:], first_scale[:], 0, HALF)
+        project(0, first_codes[:], first_scale[:], HALF, T)
+        round_w_pair1(nc.scalar.copy, 0)
+        round_w_pair0(nc.vector.tensor_copy, rest_bf16[:, 0 : P * PACK], 1, 0, L_HALF)
+        round_w_pair1(nc.vector.tensor_copy, 1)
+        nc.vector.quantize_mx(
+            out=rest_codes[:, 0:P].bitcast(FP8X4), scales=rest_scale[:, 0:P], in_=rest_bf16[:, 0 : P * PACK]
+        )
+        nc.vector.quantize_mx(
+            out=rest_codes[:, P:].bitcast(FP8X4), scales=rest_scale[:, P:], in_=rest_bf16[:, P * PACK :]
+        )
 
-        def project_rest():
-            for g in range(1, 4):
-                project(g, wq[:, (g - 1) * P : g * P], ws[:, (g - 1) * P : g * P], 0, T)
-            nc.scalar.copy(ys[2][:, T:], ys[3][:, 0:SPARE])
-            nc.scalar.copy(ys[3][:, T:], ys[2][:, T:])
-
-        def gather(prod, g, d, lo, hi):
-            nc.vector.tensor_tensor(prod, ys[g][:].indirect(lists[d][:, lo // 16 : hi // 16]), gates[d][:, lo:hi], ALU.mult)
-
-        own01 = keep.tile([P, VB, 2, P], F32, name="own01")
-        sum01 = keep.tile([P, VB, 2, P], F32, name="sum01")
-        own23 = [keep.tile([P, VB, P], F32, name="own%d" % t) for t in (2, 3)]
-        sum23 = [keep.tile([P, VB, P], F32, name="sum%d" % t) for t in (2, 3)]
-        stay = keep.tile([P, VB], F32, name="stay")
-
-        def make_stay():
-            bank = new_bank("turn")
-            for d in range(D):
-                nc.tensor.matmul(bank[:, 0:P], gate_rows[:, d, :], ident[:], start=d == 0, stop=d == D - 1, is_transpose=True)
-            nc.scalar.activation(stay[:], bank[:, 0:VB], ACT.Copy, bias=1.0, scale=-1.0)
+        own01 = keep.tile([P, BLOCKS, PAIR, P], F32, name="own01")
+        sums01 = keep.tile([P, BLOCKS, PAIR, P], F32, name="sums01")
+        own23 = [keep.tile([P, BLOCKS, P], F32, name="own%d" % t) for t in (2, 3)]
+        sums23 = [keep.tile([P, BLOCKS, P], F32, name="sums%d" % t) for t in (2, 3)]
+        stay = keep.tile([P, BLOCKS], F32, name="stay")
 
         def own_term(g):
-            bank = new_bank("turn")
-            transpose_into(bank, lambda b: ys[g][:, b * P : (b + 1) * P], True, True)
-            for b in range(VB):
+            bank = new_bank("turned")
+            transpose_blocks(bank, ys[g], True, True)
+            for b in range(BLOCKS):
                 src = bank[:, b * P : (b + 1) * P]
                 if g < 2:
-                    nc.scalar.activation(own01[:, b, :, 64 * g : 64 * g + 64], src.rearrange("p (l t) -> p t l", t=2), ACT.Copy, scale=stay[:, b : b + 1])
+                    dst = own01[:, b, :, L_HALF * g : L_HALF * (g + 1)]
+                    src = src.rearrange("p (l t) -> p t l", t=PAIR)
                 else:
-                    nc.scalar.activation(own23[g - 2][:, b, :], src, ACT.Copy, scale=stay[:, b : b + 1])
+                    dst = own23[g - 2][:, b, :]
+                nc.scalar.activation(dst, src, ACT.Copy, scale=stay[:, b : b + 1])
 
-        banks = {}
+        def gather(dst, g, d, lo, hi):
+            offsets = lists[d][:, lo // PER_COLUMN : hi // PER_COLUMN]
+            nc.vector.tensor_tensor(dst, ys[g][:].indirect(offsets), gates[d][:, lo:hi], ALU.mult)
 
-        def neighbour(g, d, last):
+        sum_bank = {}
+
+        def neighbour(g, d):
             if d == 0:
-                banks[g] = psum.tile([P, T], F32, name="sums", tag="sums", bufs=3)
+                sum_bank[g] = psum.tile([P, T], F32, name="sum_bank", tag="sum_bank", bufs=SUM_BANKS)
             prod = ring.tile([P, T], F32, name="prod", tag="prod")
             gather(prod[:], g, d, 0, T)
-            transpose_into(banks[g], lambda b: prod[:, b * P : (b + 1) * P], d == 0, last)
+            last_transposed = D - 1 if g < 2 else D - 2
+            transpose_blocks(sum_bank[g], prod, d == 0, d == last_transposed)
 
         def empty_sums(g):
             if g < 2:
-                nc.scalar.copy(sum01[:, :, :, 64 * g : 64 * g + 64], banks[g][:].rearrange("p (b l t) -> p b t l", b=VB, t=2))
+                nc.scalar.copy(
+                    sums01[:, :, :, L_HALF * g : L_HALF * (g + 1)],
+                    sum_bank[g][:].rearrange("p (b l t) -> p b t l", b=BLOCKS, t=PAIR),
+                )
             else:
                 for h in range(2):
-                    nc.scalar.copy(sum23[g - 2][:, 2 * h : 2 * h + 2, :].rearrange("p b l -> p (b l)"), banks[g][:, h * HALF : (h + 1) * HALF])
+                    nc.scalar.copy(
+                        sums23[g - 2][:, 2 * h : 2 * h + 2, :].rearrange("p b l -> p (b l)"),
+                        sum_bank[g][:, h * HALF : (h + 1) * HALF],
+                    )
 
-        res = [[keep.tile([P, 2, HALF], F32, name="res%d%d" % (pair, h)) for h in range(2)] for pair in range(2)]
-        out_rows = out_0.rearrange("(l t) v -> l t v", t=PACK)
+        back = {}
 
-        def turn_back(bank, pair, h, src01, src23, first):
+        def turn_back(pair, h, terms01, terms23, first):
             for i in range(4):
-                t, b = 2 * pair + i // 2, 2 * h + i % 2
-                src = src01[:, b, t, :] if pair == 0 else src23[t - 2][:, b, :]
-                nc.tensor.matmul(bank[:, i * P : (i + 1) * P], src, ident[:], start=first and i == 0, stop=not first and i == 3, is_transpose=True)
+                t, b = PAIR * pair + i // 2, 2 * h + i % 2
+                src = terms01[:, b, t, :] if pair == 0 else terms23[t - 2][:, b, :]
+                transpose(back[pair, h][:, i * P : (i + 1) * P], src, first and i == 0, not first and i == 3)
 
         def back_own(pair, h):
-            bank = new_bank("back")
-            turn_back(bank, pair, h, own01, own23, True)
-            return bank
+            back[pair, h] = new_bank("back")
+            turn_back(pair, h, own01, own23, True)
 
-        def back_sum(bank, pair, h):
-            turn_back(bank, pair, h, sum01, sum23, False)
+        def back_sums(pair, h):
+            turn_back(pair, h, sums01, sums23, False)
+
+        res = [[keep.tile([P, PAIR, HALF], F32, name="res%d%d" % (pair, h)) for h in range(2)] for pair in range(2)]
+        out_rows = out_0.rearrange("(l t) v -> l t v", t=PACK)
+        res_bf16 = [keep.tile([P, HALF * PACK], BF16, name="res_bf16_%d" % h, align_bytes=64) for h in range(2)]
 
         def store(pair, h):
-            nc.sync.dma_start(out=out_rows[:, 2 * pair : 2 * pair + 2, h * HALF : (h + 1) * HALF], in_=res[pair][h][:])
+            nc.sync.dma_start(
+                out=out_rows[:, PAIR * pair : PAIR * (pair + 1), h * HALF : (h + 1) * HALF], in_=res[pair][h][:]
+            )
 
-        rounded = [keep.tile([P, HALF * PACK], BF16, name="rounded%d" % h, align_bytes=64) for h in range(2)]
+        def round_res(copy, pair, h):
+            copy(
+                out=res_bf16[h][:].rearrange("p (c t) -> p c t", t=PACK)[:, :, PAIR * pair : PAIR * (pair + 1)],
+                in_=res[pair][h][:].rearrange("p t c -> p c t"),
+            )
 
-        def round_pair(copy, pair, h):
-            copy(out=rounded[h][:].rearrange("p (c t) -> p c t", t=PACK)[:, :, 2 * pair : 2 * pair + 2], in_=res[pair][h][:].rearrange("p t c -> p c t"))
+        gate_sum = new_bank("turned")
+        for d in range(D):
+            transpose(gate_sum[:, 0:P], gate_rows[:, d, :], d == 0, d == D - 1)
+        nc.scalar.activation(stay[:], gate_sum[:, 0:BLOCKS], ACT.Copy, bias=1.0, scale=-1.0)
 
-        def finish(bank, h):
-            nc.scalar.copy(res[0][h][:].rearrange("p t c -> p (t c)"), bank[:])
-            store(0, h)
-
-        make_stay()
-        back = {}
         own_term(0)
-        project_rest()
+        for g in range(1, 4):
+            cols = slice((g - 1) * P, g * P)
+            project(g, rest_codes[:, cols], rest_scale[:, cols], 0, T)
+        nc.scalar.copy(ys[2][:, T:], ys[3][:, 0:SPARE])
+        nc.scalar.copy(ys[3][:, T:], ys[2][:, T:])
         own_term(1)
-        neighbour(0, 0, False)
+        neighbour(0, 0)
         own_term(2)
-        neighbour(0, 1, False)
-        neighbour(0, 2, True)
+        neighbour(0, 1)
+        neighbour(0, 2)
         empty_sums(0)
-        back[0, 0] = back_own(0, 0)
-        back[0, 1] = back_own(0, 1)
-        neighbour(1, 0, False)
-        neighbour(1, 1, False)
-        neighbour(1, 2, True)
+        for h in range(2):
+            back_own(0, h)
+        for d in range(D):
+            neighbour(1, d)
         empty_sums(1)
         own_term(3)
-        back_sum(back[0, 0], 0, 0)
-        finish(back[0, 0], 0)
-        back_sum(back[0, 1], 0, 1)
-        finish(back[0, 1], 1)
-        round_pair(nc.scalar.copy, 0, 0)
-        round_pair(nc.scalar.copy, 0, 1)
-        neighbour(2, 0, False)
-        back[1, 0] = back_own(1, 0)
-        neighbour(3, 0, False)
-        back[1, 1] = back_own(1, 1)
-        neighbour(2, 1, True)
-        empty_sums(2)
-        neighbour(3, 1, True)
-        empty_sums(3)
-        back_sum(back[1, 0], 1, 0)
-        back_sum(back[1, 1], 1, 1)
+        for h in range(2):
+            back_sums(0, h)
+            nc.scalar.copy(res[0][h][:].rearrange("p t c -> p (t c)"), back[0, h][:])
+            store(0, h)
+        for h in range(2):
+            round_res(nc.scalar.copy, 0, h)
 
-        last = [keep.tile([P, 2, HALF], F32, name="last%d" % h) for h in range(2)]
+        neighbour(2, 0)
+        back_own(1, 0)
+        neighbour(3, 0)
+        back_own(1, 1)
+        for g in (2, 3):
+            neighbour(g, 1)
+            empty_sums(g)
+        for h in range(2):
+            back_sums(1, h)
+
+        third = [keep.tile([P, PAIR, HALF], F32, name="third%d" % h) for h in range(2)]
         for h in range(2):
             for g in (2, 3):
-                gather(last[h][:, g - 2, :], g, 2, h * HALF, (h + 1) * HALF)
+                gather(third[h][:, g - 2, :], g, D - 1, h * HALF, (h + 1) * HALF)
         for h in range(2):
-            nc.vector.tensor_tensor(res[1][h][:].rearrange("p t c -> p (t c)"), back[1, h][:], last[h][:].rearrange("p t c -> p (t c)"), ALU.add)
+            nc.vector.tensor_tensor(
+                res[1][h][:].rearrange("p t c -> p (t c)"),
+                back[1, h][:],
+                third[h][:].rearrange("p t c -> p (t c)"),
+                ALU.add,
+            )
             store(1, h)
-        round_pair(nc.scalar.copy, 1, 0)
-        round_pair(nc.vector.tensor_copy, 1, 1)
-        codes = keep.tile([P, T], U32, name="codes", align_bytes=64)
-        scales = keep.tile([P, T], U8, name="scales", align_bytes=64)
+        round_res(nc.scalar.copy, 1, 0)
+        round_res(nc.vector.tensor_copy, 1, 1)
+
+        res_codes = keep.tile([P, T], U32, name="res_codes", align_bytes=64)
+        res_scale = keep.tile([P, T], U8, name="res_scale", align_bytes=64)
         words_out = out_1[0].rearrange("p n t -> p (n t)").bitcast(I32)
         for h in range(2):
             cols = slice(h * HALF, (h + 1) * HALF)
-            nc.vector.quantize_mx(out=codes[:, cols].bitcast(FP8X4), scales=scales[:, cols], in_=rounded[h][:])
-            nc.sync.dma_start(out=words_out[:, cols], in_=codes[:, cols].bitcast(I32))
-        for q in range(4):
+            nc.vector.quantize_mx(out=res_codes[:, cols].bitcast(FP8X4), scales=res_scale[:, cols], in_=res_bf16[h][:])
+            nc.sync.dma_start(out=words_out[:, cols], in_=res_codes[:, cols].bitcast(I32))
+        for q in range(QUADRANTS):
             queue = nc.scalar if q % 2 == 0 else nc.sync
-            queue.dma_start(out=out_2[0, 4 * q : 4 * q + 4, :].bitcast(I32), in_=scales[32 * q : 32 * q + 4, :].bitcast(I32))
+            queue.dma_start(
+                out=out_2[0, 4 * q : 4 * q + 4, :].bitcast(I32), in_=res_scale[32 * q : 32 * q + 4, :].bitcast(I32)
+            )

from contextlib import ExitStack

import concourse.mybir as mybir
from concourse.masks import make_identity

K, T, D, N = 512, 512, 3, 512
FLOPS = 2 * K * T * N + 9 * N * T

F32 = mybir.dt.float32
BF16 = mybir.dt.bfloat16
I32 = mybir.dt.int32
U32 = mybir.dt.uint32
U16 = mybir.dt.uint16
U8 = mybir.dt.uint8
FP8X4 = mybir.dt.float8_e4m3fn_x4
ACT = mybir.ActivationFunctionType
ALU = mybir.AluOpType

P = 128
PACK = 4
PAIR = 2
QUADRANTS = 4
BLOCKS = T // P
HALF = T // 2
L_HALF = P // 2
PER_COLUMN = 16
SPARE = 8
L_VECTOR = 40
TRANSPOSED_TERMS = 10
SUM_BANKS = 3
OTHER_BANKS = 5


def tile_picked_wgrand_relu_lo_kernel(
    tc, x_words, x_scales, w1, gate, pos1, pos2, pos3, out_0, out_1, out_2
):
    nc = tc.nc
    with ExitStack() as ctx:
        keep = ctx.enter_context(tc.tile_pool(name="keep", bufs=1))
        ring = ctx.enter_context(tc.tile_pool(name="ring", bufs=TRANSPOSED_TERMS))
        psum = ctx.enter_context(tc.psum_pool(name="psum", bufs=1))

        x_scale = keep.tile([P, T], U8, name="x_scale", align_bytes=64)
        nc.gpsimd.memset(x_scale[:].bitcast(I32), 0)
        w_rows = w1.rearrange("(p j) m -> p j m", j=PACK)
        w_raw = [keep.tile([P, PACK, HALF], F32, name="w_raw%d" % h) for h in range(2)]
        nc.sync.dma_start(out=w_raw[0][:], in_=w_rows[:, :, 0:HALF])
        x_codes = keep.tile([P, T], U32, name="x_codes", align_bytes=64)
        for q in range(QUADRANTS):
            nc.sync.dma_start(
                out=x_scale[32 * q : 32 * q + 4, :].bitcast(I32), in_=x_scales[0, 4 * q : 4 * q + 4, :].bitcast(I32)
            )
        gate_rows = keep.tile([P, D, P], F32, name="gate_rows")
        nc.gpsimd.memset(gate_rows[:], 0.0)
        nc.sync.dma_start(out=gate_rows[0:BLOCKS, :, :], in_=gate[:, 0, :].rearrange("d (b c) -> b d c", b=BLOCKS))
        nc.sync.dma_start(out=x_codes[:].bitcast(I32), in_=x_words[0].rearrange("p n t -> p (n t)").bitcast(I32))
        lists = [keep.tile([P, T // PER_COLUMN], U16, name="list%d" % d) for d in range(D)]
        gates = [keep.tile([P, T], F32, name="gate%d" % d) for d in range(D)]
        nc.sync.dma_start(out=w_raw[1][:], in_=w_rows[:, :, HALF:N])
        for d, pos in enumerate((pos1, pos2, pos3)):
            nc.sync.dma_start(lists[d][:], pos)
            nc.sync.dma_start(out=gates[d][:], in_=gate[d])

        ident = keep.tile([P, P], F32, name="ident")
        make_identity(nc, ident[:])

        ys = [keep.tile([P, T + SPARE], F32, name="y%d" % g) for g in range(4)]
        nc.scalar.activation(ys[0][:, T:], ident[:, 0:SPARE], ACT.Relu)
        nc.gpsimd.memset(ys[1][:, T:], 0.0)

        def new_bank(name):
            return psum.tile([P, T], F32, name=name, tag="bank", bufs=OTHER_BANKS)

        def transpose(dst, src, start, stop):
            nc.tensor.matmul(dst, src, ident[:], start=start, stop=stop, is_transpose=True)

        def transpose_blocks(bank, src, first, last):
            for b in range(BLOCKS):
                cols = slice(b * P, (b + 1) * P)
                transpose(bank[:, cols], src[:, cols], first and b == 0, last and b == BLOCKS - 1)

        first_bf16 = keep.tile([P, P * PACK], BF16, name="first_bf16", align_bytes=64)
        first_codes = keep.tile([P, P], U32, name="first_codes", align_bytes=64)
        first_scale = keep.tile([P, P], U8, name="first_scale", align_bytes=64)
        rest_bf16 = keep.tile([P, 3 * P * PACK], BF16, name="rest_bf16", align_bytes=64)
        rest_codes = keep.tile([P, 3 * P], U32, name="rest_codes", align_bytes=64)
        rest_scale = keep.tile([P, 3 * P], U8, name="rest_scale", align_bytes=64)
        w_cols = [w_raw[h][:].rearrange("p j (l t) -> p l t j", t=PACK) for h in range(2)]

        def round_w_pair0(copy, dst, h, lo, hi):
            copy(
                out=dst.rearrange("p (l t j) -> p l t j", t=PAIR, j=PACK)[:, lo:hi, :, :],
                in_=w_cols[h][:, lo:hi, 0:PAIR, :],
            )

        def round_w_pair1(copy, h):
            dst = rest_bf16[:, P * PACK :].rearrange("p (t l j) -> p l t j", t=PAIR, j=PACK)
            copy(out=dst[:, L_HALF * h : L_HALF * (h + 1), :, :], in_=w_cols[h][:, :, PAIR:PACK, :])

        def project(g, w_codes, w_scale, lo, hi):
            acc = new_bank("acc")
            nc.tensor.matmul_mx(
                out=acc[:, 0 : hi - lo],
                lhsT=w_codes.bitcast(FP8X4),
                lhsT_scale=w_scale,
                rhs=x_codes[:, lo:hi].bitcast(FP8X4),
                rhs_scale=x_scale[:, lo:hi],
                start=True,
                stop=True,
            )
            nc.scalar.activation(ys[g][:, lo:hi], acc[:, 0 : hi - lo], ACT.Relu)

        round_w_pair0(nc.vector.tensor_copy, first_bf16[:], 0, 0, L_VECTOR)
        round_w_pair0(nc.scalar.copy, first_bf16[:], 0, L_VECTOR, L_HALF)
        nc.vector.quantize_mx(out=first_codes[:].bitcast(FP8X4), scales=first_scale[:], in_=first_bf16[:])
        project(0, first_codes[:], first_scale[:], 0, HALF)
        project(0, first_codes[:], first_scale[:], HALF, T)
        round_w_pair1(nc.scalar.copy, 0)
        round_w_pair0(nc.vector.tensor_copy, rest_bf16[:, 0 : P * PACK], 1, 0, L_HALF)
        round_w_pair1(nc.vector.tensor_copy, 1)
        nc.vector.quantize_mx(
            out=rest_codes[:, 0:P].bitcast(FP8X4), scales=rest_scale[:, 0:P], in_=rest_bf16[:, 0 : P * PACK]
        )
        nc.vector.quantize_mx(
            out=rest_codes[:, P:].bitcast(FP8X4), scales=rest_scale[:, P:], in_=rest_bf16[:, P * PACK :]
        )

        own01 = keep.tile([P, BLOCKS, PAIR, P], F32, name="own01")
        sums01 = keep.tile([P, BLOCKS, PAIR, P], F32, name="sums01")
        own23 = [keep.tile([P, BLOCKS, P], F32, name="own%d" % t) for t in (2, 3)]
        sums23 = [keep.tile([P, BLOCKS, P], F32, name="sums%d" % t) for t in (2, 3)]
        stay = keep.tile([P, BLOCKS], F32, name="stay")

        def own_term(g):
            bank = new_bank("turned")
            transpose_blocks(bank, ys[g], True, True)
            for b in range(BLOCKS):
                src = bank[:, b * P : (b + 1) * P]
                if g < 2:
                    dst = own01[:, b, :, L_HALF * g : L_HALF * (g + 1)]
                    src = src.rearrange("p (l t) -> p t l", t=PAIR)
                else:
                    dst = own23[g - 2][:, b, :]
                nc.scalar.activation(dst, src, ACT.Copy, scale=stay[:, b : b + 1])

        def gather(dst, g, d, lo, hi):
            offsets = lists[d][:, lo // PER_COLUMN : hi // PER_COLUMN]
            nc.vector.tensor_tensor(dst, ys[g][:].indirect(offsets), gates[d][:, lo:hi], ALU.mult)

        sum_bank = {}

        def neighbour(g, d):
            if d == 0:
                sum_bank[g] = psum.tile([P, T], F32, name="sum_bank", tag="sum_bank", bufs=SUM_BANKS)
            prod = ring.tile([P, T], F32, name="prod", tag="prod")
            gather(prod[:], g, d, 0, T)
            last_transposed = D - 1 if g < 2 else D - 2
            transpose_blocks(sum_bank[g], prod, d == 0, d == last_transposed)

        def empty_sums(g):
            if g < 2:
                nc.scalar.copy(
                    sums01[:, :, :, L_HALF * g : L_HALF * (g + 1)],
                    sum_bank[g][:].rearrange("p (b l t) -> p b t l", b=BLOCKS, t=PAIR),
                )
            else:
                for h in range(2):
                    nc.scalar.copy(
                        sums23[g - 2][:, 2 * h : 2 * h + 2, :].rearrange("p b l -> p (b l)"),
                        sum_bank[g][:, h * HALF : (h + 1) * HALF],
                    )

        back = {}

        def turn_back(pair, h, terms01, terms23, first):
            for i in range(4):
                t, b = PAIR * pair + i // 2, 2 * h + i % 2
                src = terms01[:, b, t, :] if pair == 0 else terms23[t - 2][:, b, :]
                transpose(back[pair, h][:, i * P : (i + 1) * P], src, first and i == 0, not first and i == 3)

        def back_own(pair, h):
            back[pair, h] = new_bank("back")
            turn_back(pair, h, own01, own23, True)

        def back_sums(pair, h):
            turn_back(pair, h, sums01, sums23, False)

        res = [[keep.tile([P, PAIR, HALF], F32, name="res%d%d" % (pair, h)) for h in range(2)] for pair in range(2)]
        out_rows = out_0.rearrange("(l t) v -> l t v", t=PACK)
        res_bf16 = [keep.tile([P, HALF * PACK], BF16, name="res_bf16_%d" % h, align_bytes=64) for h in range(2)]

        def store(pair, h):
            nc.sync.dma_start(
                out=out_rows[:, PAIR * pair : PAIR * (pair + 1), h * HALF : (h + 1) * HALF], in_=res[pair][h][:]
            )

        def round_res(copy, pair, h):
            copy(
                out=res_bf16[h][:].rearrange("p (c t) -> p c t", t=PACK)[:, :, PAIR * pair : PAIR * (pair + 1)],
                in_=res[pair][h][:].rearrange("p t c -> p c t"),
            )

        gate_sum = new_bank("turned")
        for d in range(D):
            transpose(gate_sum[:, 0:P], gate_rows[:, d, :], d == 0, d == D - 1)
        nc.scalar.activation(stay[:], gate_sum[:, 0:BLOCKS], ACT.Copy, bias=1.0, scale=-1.0)

        own_term(0)
        for g in range(1, 4):
            cols = slice((g - 1) * P, g * P)
            project(g, rest_codes[:, cols], rest_scale[:, cols], 0, T)
        nc.scalar.copy(ys[2][:, T:], ys[3][:, 0:SPARE])
        nc.scalar.copy(ys[3][:, T:], ys[2][:, T:])
        own_term(1)
        neighbour(0, 0)
        own_term(2)
        neighbour(0, 1)
        neighbour(0, 2)
        empty_sums(0)
        for h in range(2):
            back_own(0, h)
        for d in range(D):
            neighbour(1, d)
        empty_sums(1)
        own_term(3)
        for h in range(2):
            back_sums(0, h)
            nc.scalar.copy(res[0][h][:].rearrange("p t c -> p (t c)"), back[0, h][:])
            store(0, h)
        for h in range(2):
            round_res(nc.scalar.copy, 0, h)

        neighbour(2, 0)
        back_own(1, 0)
        neighbour(3, 0)
        back_own(1, 1)
        for g in (2, 3):
            neighbour(g, 1)
            empty_sums(g)
        for h in range(2):
            back_sums(1, h)

        third = [keep.tile([P, PAIR, HALF], F32, name="third%d" % h) for h in range(2)]
        for h in range(2):
            for g in (2, 3):
                gather(third[h][:, g - 2, :], g, D - 1, h * HALF, (h + 1) * HALF)
        for h in range(2):
            nc.vector.tensor_tensor(
                res[1][h][:].rearrange("p t c -> p (t c)"),
                back[1, h][:],
                third[h][:].rearrange("p t c -> p (t c)"),
                ALU.add,
            )
            store(1, h)
        round_res(nc.scalar.copy, 1, 0)
        round_res(nc.vector.tensor_copy, 1, 1)

        res_codes = keep.tile([P, T], U32, name="res_codes", align_bytes=64)
        res_scale = keep.tile([P, T], U8, name="res_scale", align_bytes=64)
        words_out = out_1[0].rearrange("p n t -> p (n t)").bitcast(I32)
        for h in range(2):
            cols = slice(h * HALF, (h + 1) * HALF)
            nc.vector.quantize_mx(out=res_codes[:, cols].bitcast(FP8X4), scales=res_scale[:, cols], in_=res_bf16[h][:])
            nc.sync.dma_start(out=words_out[:, cols], in_=res_codes[:, cols].bitcast(I32))
        for q in range(QUADRANTS):
            queue = nc.scalar if q % 2 == 0 else nc.sync
            queue.dma_start(
                out=out_2[0, 4 * q : 4 * q + 4, :].bitcast(I32), in_=res_scale[32 * q : 32 * q + 4, :].bitcast(I32)
            )
